import numpy as np
CORES = [113,118,241,246]
N = 4
F = 16
TK = N * F
EPS = 0.01
def setup_inputs(rng):
    return {"x": rng.standard_normal((N, 128, TK), dtype=np.float32) * (0.5 + np.abs(rng.standard_normal((1, 1, TK), dtype=np.float32)))}
def setup_inputs_big(rng):
    d = setup_inputs(rng)
    for k in ("x",): d[k] = (d[k].astype(np.float32) * 1024.0).astype(d[k].dtype)
    return d
def setup_inputs_small(rng):
    d = setup_inputs(rng)
    for k in ("x",): d[k] = (d[k].astype(np.float32) * (1 / 1024.0)).astype(d[k].dtype)
    return d
def setup_inputs_apart(rng):
    d = setup_inputs(rng)
    f = (10.0 ** rng.permutation(np.linspace(-1.5, 1.5, N))).astype(np.float32).reshape(N, 1, 1)
    for k in ("x",): d[k] = (d[k].astype(np.float32) * f).astype(d[k].dtype)
    return d
def setup_inputs_mixed(rng):
    d = setup_inputs(rng)
    f = (10.0 ** rng.uniform(-3, 3, (1, 1, TK))).astype(np.float32); shape = rng.integers(2, size=(1, 1, TK))
    for k in ("x",):
        x = d[k].astype(np.float32)
        other = x * np.where(rng.random((1, 128, TK)) < 0.5, 0.1, 1.0).astype(np.float32)
        d[k] = (np.where(shape == 1, other, x) * f).astype(d[k].dtype)
    return d
def reference(x):
    s = x.astype(np.float64).sum(axis=0)
    n = s / np.sqrt((s ** 2).sum(axis=0) / 128 + EPS)
    return {"y": np.broadcast_to(n.astype(np.float32), (N, 128, TK))}

@@ -1,0 +1,153 @@
+from concourse.bass import DstId, RemoteDMATransfer
+from concourse.mybir import AluOpType, ActivationFunctionType
+
+N = 4
+TK = 64
+EPS = 0.01
+K = 2.0 ** -22
+
+SCRATCH = {
+    "xs": ("sbuf", [128, N * TK], "float32"),
+    "cm": ("sbuf", [128, 128], "float32"),
+    "er": ("sbuf", [128, TK], "float32"),
+    "sq": ("sbuf", [128, TK], "float32"),
+    "w": ("sbuf", [128, TK], "float32"),
+    "q": ("sbuf", [128, TK], "float32"),
+    "b": ("sbuf", [128, TK], "float32"),
+    "c": ("sbuf", [128, TK], "float32"),
+    "ys": ("sbuf", [128, TK], "float32"),
+    "ps": ("psum", [128, 512], "float32"),
+    "pv1": ("psum", [128, 512], "float32"),
+    "pv2": ("psum", [128, 512], "float32"),
+    "pu": ("psum", [128, 512], "float32"),
+    "pw": ("psum", [128, 512], "float32"),
+}
+SEMAPHORES = ["ld", "st", "sent", "arr0", "arr1", "arr2", "arr3", "cst", "a1", "a2", "s", "sqd", "m1", "m2",
+              "wd", "w2d", "qd", "ud", "zd", "bd", "cd", "yd"]
+
+
+def _bits(mask):
+    return [e for e in range(mask.bit_length()) if (mask >> e) & 1]
+
+
+def _mask(engines):
+    m = 0
+    for e in engines:
+        m |= 1 << e
+    return m
+
+
+def _pow2(n):
+    p = 1
+    while p * 2 <= n:
+        p *= 2
+    return p
+
+
+def _plan(src, cores, topo):
+    others = [d for d in cores if d != src and topo.may_write(src, d)]
+    near = [d for d in others if topo.host(d) == topo.host(src) and topo.chip(d) == topo.chip(src)]
+    far = [d for d in others if d not in near]
+    far.sort(key=lambda d: (topo.die(d) != topo.die(src), d))
+    out = topo.mask(src, far[0])
+    for d in far:
+        out &= topo.mask(src, d)
+    eng = _bits(out)
+    k = _pow2(len(eng) // len(far))
+    far_plan = [(d, _mask(eng[i * k:(i + 1) * k])) for i, d in enumerate(far)]
+    near_plan = []
+    for d in near:
+        rest = [e for e in _bits(topo.mask(src, d)) if e not in eng]
+        near_plan.append((d, _mask(rest[:_pow2(len(rest))])))
+    return far_plan, near_plan
+
+
+def rank_program(g, core, T, topo):
+    rank = T.rank_of(core)
+    if rank is None:
+        return
+    S = T.sem
+    cores = list(T.cores)
+    far, near = _plan(core, cores, topo)
+
+    def slot(r):
+        return T.xs[:, r * TK:(r + 1) * TK]
+
+    def landed(d):
+        f, n = _plan(d, cores, topo)
+        m = dict(f + n)[core]
+        return S["arr%d" % T.rank_of(d)], len(_bits(m))
+
+    mine = slot(rank)
+    add, mult = AluOpType.add, AluOpType.mult
+    v, a, pe = g.vector, g.scalar, g.tensor
+
+    g.sync.dma_start(mine, T.x[:]).then_inc(S.ld, 16)
+
+    g.wait_ge(S.ld, 16)
+    sent = 0
+    trs = []
+    for d, m in far:
+        rid, pid = topo.addr(d, core)
+        trs.append(RemoteDMATransfer(dst_ids=[DstId(rid=rid, pnc=pid)], dma_engine_mask=m,
+                                     remote_sem=S["arr%d" % rank], src=mine, dst=mine))
+        sent += len(_bits(m))
+    g.remote_dma_fused(trs, local_sem=S.sent)
+    for d, m in near:
+        rid, pid = topo.addr(d, core)
+        g.remote_dma(mine, mine, S["arr%d" % rank], S.sent, pid, rid, m)
+        sent += len(_bits(m))
+    g.wait_ge(S.sent, sent)
+
+    v.memset(T.cm[:], 1.0 / 128.0).then_inc(S.cst, 1)
+    v.memset(T.er[0:1, :], 128.0 * EPS * K * K).then_inc(S.cst, 1)
+    s_ = T.ps[:, 0:TK]
+    v1, v2 = T.pv1[:, 0:TK], T.pv2[:, 0:TK]
+    u_, z_ = T.pu[:, 0:TK], T.pu[:, TK:2 * TK]
+    w2 = T.pw[:, 0:TK]
+    pe.wait_ge(S.cst, 2)
+    pe.matmul(v1, T.cm[0:1, :], T.er[0:1, :], True, False)
+    pe.matmul(v2, T.cm[0:1, :], T.er[0:1, :], True, False)
+
+    order = [d for d, _ in near] + [d for d, _ in far]
+    steps = [S.a1, S.a2, S.s]
+    v.wait_ge(S.ld, 16)
+    prev = None
+    for i, d in enumerate(order):
+        sem, cnt = landed(d)
+        v.wait_ge(sem, cnt)
+        if prev is not None:
+            v.wait_ge(prev, 1)
+        v.tensor_tensor(s_, mine if i == 0 else s_, slot(T.rank_of(d)), add).then_inc(steps[i], 1)
+        prev = steps[i]
+
+    a.wait_ge(S.s, 1)
+    a.activation(T.sq[:], s_, ActivationFunctionType.Square, scale=K).then_inc(S.sqd, 1)
+    pe.wait_ge(S.sqd, 1)
+    pe.matmul(v1, T.cm[:], T.sq[:], False, True).then_inc(S.m1, 1)
+    pe.matmul(v2, T.cm[:], T.sq[:], False, True).then_inc(S.m2, 1)
+
+    a.wait_ge(S.m1, 1)
+    a.activation(T.w[:], v1, ActivationFunctionType.Sqrt).then_inc(S.wd, 1)
+    a.wait_ge(S.wd, 1)
+    a.activation(w2, T.w[:], ActivationFunctionType.Square).then_inc(S.w2d, 1)
+
+    v.wait_ge(S.m2, 1)
+    v.reciprocal(T.q[:], v2).then_inc(S.qd, 1)
+    v.wait_ge(S.qd, 1)
+    v.wait_ge(S.s, 1)
+    v.tensor_tensor(u_, s_, T.q[:], mult).then_inc(S.ud, 1)
+    v.wait_ge(S.ud, 1)
+    v.wait_ge(S.wd, 1)
+    v.tensor_tensor(z_, u_, T.w[:], mult).then_inc(S.zd, 1)
+    v.wait_ge(S.w2d, 1)
+    v.tensor_tensor(T.b[:], w2, T.q[:], mult).then_inc(S.bd, 1)
+    v.wait_ge(S.bd, 1)
+    v.tensor_scalar(T.c[:], T.b[:], -0.5 * K, 1.5 * K, mult, add).then_inc(S.cd, 1)
+    v.wait_ge(S.cd, 1)
+    v.wait_ge(S.zd, 1)
+    v.tensor_tensor(T.ys[:], z_, T.c[:], mult).then_inc(S.yd, 1)
+
+    g.sync.wait_ge(S.yd, 1)
+    g.sync.dma_start(T.y[:], T.ys[:]).then_inc(S.st, 16)
+    g.sync.wait_ge(S.st, 16)

@@ -1,29 +1,50 @@
+import math
 from concourse.bass import DstId, RemoteDMATransfer
 from concourse.mybir import AluOpType, ActivationFunctionType
 
 N = 4
 TK = 64
 EPS = 0.01
-K = 2.0 ** -22
+KE = 30
+K = 2.0 ** -KE
+
+E0 = -6.5
+HS = (121.0 - E0) / 253.0
+A = 0.26247634
+TOP = (-1.73475682, 4.01621331)
+LN2 = math.log(2.0)
+AL = math.sqrt(0.375 * K)
 
 SCRATCH = {
     "xs": ("sbuf", [128, N * TK], "float32"),
     "cm": ("sbuf", [128, 128], "float32"),
     "er": ("sbuf", [128, TK], "float32"),
+    "pn": ("sbuf", [128, 1], "float32"),
+    "dd": ("sbuf", [128, 1], "float32"),
+    "thr0": ("sbuf", [128, 1], "float32"),
+    "thr1": ("sbuf", [128, 1], "float32"),
+    "col0": ("sbuf", [128, 1], "float32"),
+    "col1": ("sbuf", [128, 1], "float32"),
+    "fac0": ("sbuf", [128, 1], "float32"),
+    "fac1": ("sbuf", [128, 1], "float32"),
+    "kc0": ("sbuf", [128, 128], "bfloat16"),
+    "kc1": ("sbuf", [128, 128], "bfloat16"),
+    "h0": ("sbuf", [128, TK], "bfloat16"),
+    "h1": ("sbuf", [128, TK], "bfloat16"),
+    "ss": ("sbuf", [128, TK], "float32"),
     "sq": ("sbuf", [128, TK], "float32"),
-    "w": ("sbuf", [128, TK], "float32"),
-    "q": ("sbuf", [128, TK], "float32"),
+    "a": ("sbuf", [128, TK], "float32"),
     "b": ("sbuf", [128, TK], "float32"),
+    "g2": ("sbuf", [128, TK], "float32"),
     "c": ("sbuf", [128, TK], "float32"),
     "ys": ("sbuf", [128, TK], "float32"),
     "ps": ("psum", [128, 512], "float32"),
-    "pv1": ("psum", [128, 512], "float32"),
-    "pv2": ("psum", [128, 512], "float32"),
+    "pv": ("psum", [128, 512], "float32"),
+    "pr": ("psum", [128, 512], "float32"),
     "pu": ("psum", [128, 512], "float32"),
-    "pw": ("psum", [128, 512], "float32"),
 }
-SEMAPHORES = ["ld", "st", "sent", "arr0", "arr1", "arr2", "arr3", "cst", "a1", "a2", "s", "sqd", "m1", "m2",
-              "wd", "w2d", "qd", "ud", "zd", "bd", "cd", "yd"]
+SEMAPHORES = ["ld", "st", "sent", "arr0", "arr1", "arr2", "arr3", "cst", "iod", "expd", "dd1", "fd", "kcd",
+              "a1", "a2", "s", "sqd", "m1", "hd", "m2", "ad", "bd", "g2d", "zd", "cd", "yd"]
 
 
 def _bits(mask):
@@ -79,11 +100,13 @@ def rank_program(g, core, T, topo):
         return S["arr%d" % T.rank_of(d)], len(_bits(m))
 
     mine = slot(rank)
-    add, mult = AluOpType.add, AluOpType.mult
+    add, mult, sub = AluOpType.add, AluOpType.mult, AluOpType.subtract
+    Exp, Square = ActivationFunctionType.Exp, ActivationFunctionType.Square
     v, a, pe = g.vector, g.scalar, g.tensor
 
     g.sync.dma_start(mine, T.x[:]).then_inc(S.ld, 16)
 
+    g.iota(T.pn[:], [[0, 1]], 0, 1, allow_small_or_imprecise_dtypes=True).then_inc(S.iod, 1)
     g.wait_ge(S.ld, 16)
     sent = 0
     trs = []
@@ -99,15 +122,29 @@ def rank_program(g, core, T, topo):
         sent += len(_bits(m))
     g.wait_ge(S.sent, sent)
 
+    s_run = T.ps[:, 0:TK]
+    pv, pr, z_ = T.pv[:, 0:TK], T.pr[:, 0:TK], T.pu[:, 0:TK]
+    sets = ((T.thr0, T.col0, T.fac0, T.kc0, T.h0), (T.thr1, T.col1, T.fac1, T.kc1, T.h1))
     v.memset(T.cm[:], 1.0 / 128.0).then_inc(S.cst, 1)
     v.memset(T.er[0:1, :], 128.0 * EPS * K * K).then_inc(S.cst, 1)
-    s_ = T.ps[:, 0:TK]
-    v1, v2 = T.pv1[:, 0:TK], T.pv2[:, 0:TK]
-    u_, z_ = T.pu[:, 0:TK], T.pu[:, TK:2 * TK]
-    w2 = T.pw[:, 0:TK]
     pe.wait_ge(S.cst, 2)
-    pe.matmul(v1, T.cm[0:1, :], T.er[0:1, :], True, False)
-    pe.matmul(v2, T.cm[0:1, :], T.er[0:1, :], True, False)
+    pe.matmul(pv, T.cm[0:1, :], T.er[0:1, :], True, False)
+    a.wait_ge(S.iod, 1)
+    for i, (thr, col, fac, kc, h) in enumerate(sets):
+        e0 = E0 + i * HS - 2 * KE
+        a.activation(thr[:], T.pn[:], Exp, bias=e0 * LN2, scale=2.0 * HS * LN2).then_inc(S.expd, 1)
+        a.activation(col[:], T.pn[:], Exp, bias=math.log(128.0 * A) - 1.5 * e0 * LN2,
+                     scale=-3.0 * HS * LN2).then_inc(S.expd, 1)
+    v.wait_ge(S.iod, 1)
+    v.tensor_scalar(T.dd[:], T.pn[:], -126.0, 0.0, add, AluOpType.max).then_inc(S.dd1, 1)
+    v.wait_ge(S.dd1, 1)
+    for i, (thr, col, fac, kc, h) in enumerate(sets):
+        v.tensor_scalar(fac[:], T.dd[:], 1.0 - TOP[i] / A, -1.0, mult, add).then_inc(S.fd, 1)
+    v.wait_ge(S.fd, 2)
+    v.wait_ge(S.cst, 2)
+    v.wait_ge(S.expd, 4)
+    for thr, col, fac, kc, h in sets:
+        v.tensor_scalar(kc[:], T.cm[:], col[:], fac[:], mult, mult).then_inc(S.kcd, 1)
 
     order = [d for d, _ in near] + [d for d, _ in far]
     steps = [S.a1, S.a2, S.s]
@@ -118,32 +155,31 @@ def rank_program(g, core, T, topo):
         v.wait_ge(sem, cnt)
         if prev is not None:
             v.wait_ge(prev, 1)
-        v.tensor_tensor(s_, mine if i == 0 else s_, slot(T.rank_of(d)), add).then_inc(steps[i], 1)
+        v.tensor_tensor(T.ss[:] if i == len(order) - 1 else s_run, mine if i == 0 else s_run,
+                        slot(T.rank_of(d)), add).then_inc(steps[i], 1)
         prev = steps[i]
 
     a.wait_ge(S.s, 1)
-    a.activation(T.sq[:], s_, ActivationFunctionType.Square, scale=K).then_inc(S.sqd, 1)
+    a.activation(T.sq[:], T.ss[:], Square, scale=K).then_inc(S.sqd, 1)
     pe.wait_ge(S.sqd, 1)
-    pe.matmul(v1, T.cm[:], T.sq[:], False, True).then_inc(S.m1, 1)
-    pe.matmul(v2, T.cm[:], T.sq[:], False, True).then_inc(S.m2, 1)
-
-    a.wait_ge(S.m1, 1)
-    a.activation(T.w[:], v1, ActivationFunctionType.Sqrt).then_inc(S.wd, 1)
-    a.wait_ge(S.wd, 1)
-    a.activation(w2, T.w[:], ActivationFunctionType.Square).then_inc(S.w2d, 1)
-
-    v.wait_ge(S.m2, 1)
-    v.reciprocal(T.q[:], v2).then_inc(S.qd, 1)
-    v.wait_ge(S.qd, 1)
+    pe.matmul(pv, T.cm[:], T.sq[:], False, True).then_inc(S.m1, 1)
+    v.wait_ge(S.m1, 1)
+    for thr, col, fac, kc, h in sets:
+        v.tensor_scalar(h[:], pv, thr[:], 0.0, sub, AluOpType.min).then_inc(S.hd, 1)
+    pe.wait_ge(S.kcd, 2)
+    pe.wait_ge(S.hd, 2)
+    pe.matmul(pr, T.kc0[:], T.h0[:], True, False)
+    pe.matmul(pr, T.kc1[:], T.h1[:], False, True).then_inc(S.m2, 1)
+    a.wait_ge(S.m2, 1)
+    a.activation(T.a[:], pr, Square).then_inc(S.ad, 1)
+    v.wait_ge(S.ad, 1)
+    v.tensor_tensor(T.b[:], pv, T.a[:], mult).then_inc(S.bd, 1)
+    a.wait_ge(S.bd, 1)
+    a.activation(T.g2[:], T.b[:], Square, bias=-5.0 / 3.0 * AL, scale=AL).then_inc(S.g2d, 1)
     v.wait_ge(S.s, 1)
-    v.tensor_tensor(u_, s_, T.q[:], mult).then_inc(S.ud, 1)
-    v.wait_ge(S.ud, 1)
-    v.wait_ge(S.wd, 1)
-    v.tensor_tensor(z_, u_, T.w[:], mult).then_inc(S.zd, 1)
-    v.wait_ge(S.w2d, 1)
-    v.tensor_tensor(T.b[:], w2, T.q[:], mult).then_inc(S.bd, 1)
-    v.wait_ge(S.bd, 1)
-    v.tensor_scalar(T.c[:], T.b[:], -0.5 * K, 1.5 * K, mult, add).then_inc(S.cd, 1)
+    v.tensor_tensor(z_, pr, T.ss[:], mult).then_inc(S.zd, 1)
+    v.wait_ge(S.g2d, 1)
+    v.tensor_scalar(T.c[:], T.g2[:], 5.0 / 6.0 * K, None, add).then_inc(S.cd, 1)
     v.wait_ge(S.cd, 1)
     v.wait_ge(S.zd, 1)
     v.tensor_tensor(T.ys[:], z_, T.c[:], mult).then_inc(S.yd, 1)

@@ -13,7 +13,6 @@ HS = (121.0 - E0) / 253.0
 A = 0.26247634
 TOP = (-1.73475682, 4.01621331)
 LN2 = math.log(2.0)
-AL = math.sqrt(0.375 * K)
 
 SCRATCH = {
     "xs": ("sbuf", [128, N * TK], "float32"),
@@ -33,18 +32,18 @@ SCRATCH = {
     "h1": ("sbuf", [128, TK], "bfloat16"),
     "ss": ("sbuf", [128, TK], "float32"),
     "sq": ("sbuf", [128, TK], "float32"),
-    "a": ("sbuf", [128, TK], "float32"),
-    "b": ("sbuf", [128, TK], "float32"),
-    "g2": ("sbuf", [128, TK], "float32"),
-    "c": ("sbuf", [128, TK], "float32"),
+    "d0": ("sbuf", [128, 4 * TK], "float32"),
+    "d1": ("sbuf", [128, 4 * TK], "float32"),
+    "d2": ("sbuf", [128, 4 * TK], "float32"),
     "ys": ("sbuf", [128, TK], "float32"),
     "ps": ("psum", [128, 512], "float32"),
     "pv": ("psum", [128, 512], "float32"),
     "pr": ("psum", [128, 512], "float32"),
+    "pr2": ("psum", [128, 512], "float32"),
     "pu": ("psum", [128, 512], "float32"),
 }
 SEMAPHORES = ["ld", "st", "sent", "arr0", "arr1", "arr2", "arr3", "cst", "iod", "expd", "dd1", "fd", "kcd",
-              "a1", "a2", "s", "sqd", "m1", "hd", "m2", "ad", "bd", "g2d", "zd", "cd", "yd"]
+              "a1", "a2", "s", "sqd", "m1", "hd", "m2", "m3", "cs2", "shd", "ad", "zd", "scd", "yd"]
 
 
 def _bits(mask):
@@ -94,6 +93,9 @@ def rank_program(g, core, T, topo):
     def slot(r):
         return T.xs[:, r * TK:(r + 1) * TK]
 
+    def every4(t, k):
+        return t[:, k:4 * TK:4]
+
     def landed(d):
         f, n = _plan(d, cores, topo)
         m = dict(f + n)[core]
@@ -123,10 +125,14 @@ def rank_program(g, core, T, topo):
     g.wait_ge(S.sent, sent)
 
     s_run = T.ps[:, 0:TK]
-    pv, pr, z_ = T.pv[:, 0:TK], T.pr[:, 0:TK], T.pu[:, 0:TK]
+    pv, pr, pr2, z_ = T.pv[:, 0:TK], T.pr[:, 0:TK], T.pr2[:, 0:TK], T.pu[:, 0:TK]
     sets = ((T.thr0, T.col0, T.fac0, T.kc0, T.h0), (T.thr1, T.col1, T.fac1, T.kc1, T.h1))
     v.memset(T.cm[:], 1.0 / 128.0).then_inc(S.cst, 1)
     v.memset(T.er[0:1, :], 128.0 * EPS * K * K).then_inc(S.cst, 1)
+    v.memset(every4(T.d0, 0), 0.0).then_inc(S.cs2, 1)
+    v.memset(every4(T.d1, 1), -1.25 * K).then_inc(S.cs2, 1)
+    v.memset(every4(T.d1, 2), 0.0).then_inc(S.cs2, 1)
+    v.memset(every4(T.d1, 3), 1.875 * K).then_inc(S.cs2, 1)
     pe.wait_ge(S.cst, 2)
     pe.matmul(pv, T.cm[0:1, :], T.er[0:1, :], True, False)
     a.wait_ge(S.iod, 1)
@@ -170,19 +176,23 @@ def rank_program(g, core, T, topo):
     pe.wait_ge(S.hd, 2)
     pe.matmul(pr, T.kc0[:], T.h0[:], True, False)
     pe.matmul(pr, T.kc1[:], T.h1[:], False, True).then_inc(S.m2, 1)
+    pe.matmul(pr2, T.kc0[:], T.h0[:], True, False)
+    pe.matmul(pr2, T.kc1[:], T.h1[:], False, True).then_inc(S.m3, 1)
+    v.tensor_copy(every4(T.d0, 2), pv).then_inc(S.shd, 1)
+    v.tensor_scalar(every4(T.d1, 0), pv, 0.375 * K, None, mult).then_inc(S.shd, 1)
     a.wait_ge(S.m2, 1)
-    a.activation(T.a[:], pr, Square).then_inc(S.ad, 1)
-    v.wait_ge(S.ad, 1)
-    v.tensor_tensor(T.b[:], pv, T.a[:], mult).then_inc(S.bd, 1)
-    a.wait_ge(S.bd, 1)
-    a.activation(T.g2[:], T.b[:], Square, bias=-5.0 / 3.0 * AL, scale=AL).then_inc(S.g2d, 1)
+    a.activation(every4(T.d0, 1), pr, Square).then_inc(S.ad, 1)
+    a.activation(every4(T.d0, 3), pr, Square).then_inc(S.ad, 1)
+    v.wait_ge(S.m3, 1)
     v.wait_ge(S.s, 1)
-    v.tensor_tensor(z_, pr, T.ss[:], mult).then_inc(S.zd, 1)
-    v.wait_ge(S.g2d, 1)
-    v.tensor_scalar(T.c[:], T.g2[:], 5.0 / 6.0 * K, None, add).then_inc(S.cd, 1)
-    v.wait_ge(S.cd, 1)
+    v.tensor_tensor(z_, pr2, T.ss[:], mult).then_inc(S.zd, 1)
+    v.wait_ge(S.cs2, 4)
+    v.wait_ge(S.shd, 2)
+    v.wait_ge(S.ad, 2)
+    v.tensor_tensor_scan(T.d2[:], T.d0[:], T.d1[:], 0.0, mult, add).then_inc(S.scd, 1)
+    v.wait_ge(S.scd, 1)
     v.wait_ge(S.zd, 1)
-    v.tensor_tensor(T.ys[:], z_, T.c[:], mult).then_inc(S.yd, 1)
+    v.tensor_tensor(T.ys[:], z_, every4(T.d2, 3), mult).then_inc(S.yd, 1)
 
     g.sync.wait_ge(S.yd, 1)
     g.sync.dma_start(T.y[:], T.ys[:]).then_inc(S.st, 16)

@@ -7,43 +7,39 @@ TK = 64
 EPS = 0.01
 KE = 30
 K = 2.0 ** -KE
-
-E0 = -6.5
-HS = (121.0 - E0) / 253.0
-A = 0.26247634
-TOP = (-1.73475682, 4.01621331)
+J0 = -117
 LN2 = math.log(2.0)
+C = LN2 / math.sqrt(math.pi)
+TAIL = (7.3425983, -2.68055041, 1.70019427, 0.95626398)
 
 SCRATCH = {
     "xs": ("sbuf", [128, N * TK], "float32"),
     "cm": ("sbuf", [128, 128], "float32"),
     "er": ("sbuf", [128, TK], "float32"),
     "pn": ("sbuf", [128, 1], "float32"),
-    "dd": ("sbuf", [128, 1], "float32"),
-    "thr0": ("sbuf", [128, 1], "float32"),
-    "thr1": ("sbuf", [128, 1], "float32"),
-    "col0": ("sbuf", [128, 1], "float32"),
-    "col1": ("sbuf", [128, 1], "float32"),
-    "fac0": ("sbuf", [128, 1], "float32"),
-    "fac1": ("sbuf", [128, 1], "float32"),
-    "kc0": ("sbuf", [128, 128], "bfloat16"),
-    "kc1": ("sbuf", [128, 128], "bfloat16"),
-    "h0": ("sbuf", [128, TK], "bfloat16"),
-    "h1": ("sbuf", [128, TK], "bfloat16"),
+    "two": ("sbuf", [128, 128], "float32"),
+    "zer": ("sbuf", [128, 128], "float32"),
+    "one": ("sbuf", [128, 1], "float32"),
+    "lrow": ("sbuf", [128, 128], "float32"),
+    "frow": ("sbuf", [128, 128], "float32"),
+    "nl": ("sbuf", [128, 1], "float32"),
+    "w0": ("sbuf", [128, 1], "float32"),
+    "rc": ("sbuf", [128, 1], "float32"),
+    "tt": ("sbuf", [128, 1], "float32"),
+    "wc": ("sbuf", [128, 1], "float32"),
+    "kc": ("sbuf", [128, 128], "float32"),
+    "ph": ("sbuf", [128, TK], "float32"),
     "ss": ("sbuf", [128, TK], "float32"),
     "sq": ("sbuf", [128, TK], "float32"),
-    "d0": ("sbuf", [128, 4 * TK], "float32"),
-    "d1": ("sbuf", [128, 4 * TK], "float32"),
-    "d2": ("sbuf", [128, 4 * TK], "float32"),
     "ys": ("sbuf", [128, TK], "float32"),
     "ps": ("psum", [128, 512], "float32"),
     "pv": ("psum", [128, 512], "float32"),
     "pr": ("psum", [128, 512], "float32"),
-    "pr2": ("psum", [128, 512], "float32"),
-    "pu": ("psum", [128, 512], "float32"),
+    "pc": ("psum", [128, 512], "float32"),
+    "pf": ("psum", [128, 512], "float32"),
 }
-SEMAPHORES = ["ld", "st", "sent", "arr0", "arr1", "arr2", "arr3", "cst", "iod", "expd", "dd1", "fd", "kcd",
-              "a1", "a2", "s", "sqd", "m1", "hd", "m2", "m3", "cs2", "shd", "ad", "zd", "scd", "yd"]
+SEMAPHORES = ["ld", "st", "sent", "arr0", "arr1", "arr2", "arr3", "cst", "iod", "expd", "rw", "fr", "sc", "tp", "tp2",
+              "nld", "rcd", "ttd", "wcd", "kcd", "a1", "a2", "s", "sqd", "m1", "hd", "m2", "yd"]
 
 
 def _bits(mask):
@@ -93,16 +89,13 @@ def rank_program(g, core, T, topo):
     def slot(r):
         return T.xs[:, r * TK:(r + 1) * TK]
 
-    def every4(t, k):
-        return t[:, k:4 * TK:4]
-
     def landed(d):
         f, n = _plan(d, cores, topo)
         m = dict(f + n)[core]
         return S["arr%d" % T.rank_of(d)], len(_bits(m))
 
     mine = slot(rank)
-    add, mult, sub = AluOpType.add, AluOpType.mult, AluOpType.subtract
+    add, mult = AluOpType.add, AluOpType.mult
     Exp, Square = ActivationFunctionType.Exp, ActivationFunctionType.Square
     v, a, pe = g.vector, g.scalar, g.tensor
 
@@ -125,32 +118,40 @@ def rank_program(g, core, T, topo):
     g.wait_ge(S.sent, sent)
 
     s_run = T.ps[:, 0:TK]
-    pv, pr, pr2, z_ = T.pv[:, 0:TK], T.pr[:, 0:TK], T.pr2[:, 0:TK], T.pu[:, 0:TK]
-    sets = ((T.thr0, T.col0, T.fac0, T.kc0, T.h0), (T.thr1, T.col1, T.fac1, T.kc1, T.h1))
+    pv, pr = T.pv[:, 0:TK], T.pr[:, 0:TK]
+    nt = len(TAIL)
     v.memset(T.cm[:], 1.0 / 128.0).then_inc(S.cst, 1)
     v.memset(T.er[0:1, :], 128.0 * EPS * K * K).then_inc(S.cst, 1)
-    v.memset(every4(T.d0, 0), 0.0).then_inc(S.cs2, 1)
-    v.memset(every4(T.d1, 1), -1.25 * K).then_inc(S.cs2, 1)
-    v.memset(every4(T.d1, 2), 0.0).then_inc(S.cs2, 1)
-    v.memset(every4(T.d1, 3), 1.875 * K).then_inc(S.cs2, 1)
+    v.memset(T.two[0:1, :], 2.0).then_inc(S.rw, 1)
+    v.memset(T.zer[0:1, :], 0.0).then_inc(S.rw, 1)
+    v.memset(T.one[0:1, :], 1.0).then_inc(S.rw, 1)
+    v.memset(T.frow[0:1, nt:128], 128.0).then_inc(S.fr, 1)
+    for i, t in enumerate(TAIL):
+        v.memset(T.frow[0:1, i:i + 1], 128.0 * t).then_inc(S.fr, 1)
+    v.wait_ge(S.rw, 3)
+    v.tensor_tensor_scan(T.lrow[0:1, :], T.two[0:1, :], T.zer[0:1, :], -(2.0 ** (J0 + 2 * KE - 1)), mult, add).then_inc(S.sc, 1)
     pe.wait_ge(S.cst, 2)
     pe.matmul(pv, T.cm[0:1, :], T.er[0:1, :], True, False)
+    pe.wait_ge(S.rw, 3)
+    pe.wait_ge(S.sc, 1)
+    pe.matmul(T.pc[:, 0:1], T.lrow[0:1, :], T.one[0:1, :], True, True).then_inc(S.tp, 1)
+    pe.wait_ge(S.fr, nt + 1)
+    pe.matmul(T.pf[:, 0:1], T.frow[0:1, :], T.one[0:1, :], True, True).then_inc(S.tp2, 1)
     a.wait_ge(S.iod, 1)
-    for i, (thr, col, fac, kc, h) in enumerate(sets):
-        e0 = E0 + i * HS - 2 * KE
-        a.activation(thr[:], T.pn[:], Exp, bias=e0 * LN2, scale=2.0 * HS * LN2).then_inc(S.expd, 1)
-        a.activation(col[:], T.pn[:], Exp, bias=math.log(128.0 * A) - 1.5 * e0 * LN2,
-                     scale=-3.0 * HS * LN2).then_inc(S.expd, 1)
-    v.wait_ge(S.iod, 1)
-    v.tensor_scalar(T.dd[:], T.pn[:], -126.0, 0.0, add, AluOpType.max).then_inc(S.dd1, 1)
-    v.wait_ge(S.dd1, 1)
-    for i, (thr, col, fac, kc, h) in enumerate(sets):
-        v.tensor_scalar(fac[:], T.dd[:], 1.0 - TOP[i] / A, -1.0, mult, add).then_inc(S.fd, 1)
-    v.wait_ge(S.fd, 2)
+    a.activation(T.w0[:], T.pn[:], Exp, bias=math.log(C) + 0.5 * J0 * LN2, scale=0.5 * LN2).then_inc(S.expd, 1)
+    v.wait_ge(S.tp, 1)
+    v.tensor_copy(T.nl[:], T.pc[:, 0:1]).then_inc(S.nld, 1)
+    v.wait_ge(S.expd, 1)
+    v.reciprocal(T.rc[:], T.w0[:]).then_inc(S.rcd, 1)
+    v.wait_ge(S.rcd, 1)
+    v.wait_ge(S.nld, 1)
+    v.tensor_scalar(T.tt[:], T.nl[:], T.rc[:], -0.5 * C * C * K * K, mult, mult).then_inc(S.ttd, 1)
+    v.wait_ge(S.ttd, 1)
+    v.tensor_scalar(T.wc[:], T.w0[:], 0.5, T.tt[:], mult, add).then_inc(S.wcd, 1)
+    v.wait_ge(S.wcd, 1)
+    v.wait_ge(S.tp2, 1)
     v.wait_ge(S.cst, 2)
-    v.wait_ge(S.expd, 4)
-    for thr, col, fac, kc, h in sets:
-        v.tensor_scalar(kc[:], T.cm[:], col[:], fac[:], mult, mult).then_inc(S.kcd, 1)
+    v.tensor_scalar(T.kc[:], T.cm[:], T.wc[:], T.pf[:, 0:1], mult, mult).then_inc(S.kcd, 1)
 
     order = [d for d, _ in near] + [d for d, _ in far]
     steps = [S.a1, S.a2, S.s]
@@ -169,30 +170,15 @@ def rank_program(g, core, T, topo):
     a.activation(T.sq[:], T.ss[:], Square, scale=K).then_inc(S.sqd, 1)
     pe.wait_ge(S.sqd, 1)
     pe.matmul(pv, T.cm[:], T.sq[:], False, True).then_inc(S.m1, 1)
-    v.wait_ge(S.m1, 1)
-    for thr, col, fac, kc, h in sets:
-        v.tensor_scalar(h[:], pv, thr[:], 0.0, sub, AluOpType.min).then_inc(S.hd, 1)
-    pe.wait_ge(S.kcd, 2)
-    pe.wait_ge(S.hd, 2)
-    pe.matmul(pr, T.kc0[:], T.h0[:], True, False)
-    pe.matmul(pr, T.kc1[:], T.h1[:], False, True).then_inc(S.m2, 1)
-    pe.matmul(pr2, T.kc0[:], T.h0[:], True, False)
-    pe.matmul(pr2, T.kc1[:], T.h1[:], False, True).then_inc(S.m3, 1)
-    v.tensor_copy(every4(T.d0, 2), pv).then_inc(S.shd, 1)
-    v.tensor_scalar(every4(T.d1, 0), pv, 0.375 * K, None, mult).then_inc(S.shd, 1)
-    a.wait_ge(S.m2, 1)
-    a.activation(every4(T.d0, 1), pr, Square).then_inc(S.ad, 1)
-    a.activation(every4(T.d0, 3), pr, Square).then_inc(S.ad, 1)
-    v.wait_ge(S.m3, 1)
+    a.wait_ge(S.nld, 1)
+    a.wait_ge(S.m1, 1)
+    a.activation(T.ph[:], pv, Exp, scale=T.nl[:]).then_inc(S.hd, 1)
+    pe.wait_ge(S.kcd, 1)
+    pe.wait_ge(S.hd, 1)
+    pe.matmul(pr, T.kc[:], T.ph[:], True, True).then_inc(S.m2, 1)
+    v.wait_ge(S.m2, 1)
     v.wait_ge(S.s, 1)
-    v.tensor_tensor(z_, pr2, T.ss[:], mult).then_inc(S.zd, 1)
-    v.wait_ge(S.cs2, 4)
-    v.wait_ge(S.shd, 2)
-    v.wait_ge(S.ad, 2)
-    v.tensor_tensor_scan(T.d2[:], T.d0[:], T.d1[:], 0.0, mult, add).then_inc(S.scd, 1)
-    v.wait_ge(S.scd, 1)
-    v.wait_ge(S.zd, 1)
-    v.tensor_tensor(T.ys[:], z_, every4(T.d2, 3), mult).then_inc(S.yd, 1)
+    v.tensor_tensor(T.ys[:], pr, T.ss[:], mult).then_inc(S.yd, 1)
 
     g.sync.wait_ge(S.yd, 1)
     g.sync.dma_start(T.y[:], T.ys[:]).then_inc(S.st, 16)

import math
from concourse.bass import DstId, RemoteDMATransfer
from concourse.mybir import AluOpType, ActivationFunctionType

N = 4
TK = 64
EPS = 0.01
KE = 30
K = 2.0 ** -KE
J0 = -117
LN2 = math.log(2.0)
C = LN2 / math.sqrt(math.pi)
TAIL = (7.3425983, -2.68055041, 1.70019427, 0.95626398)

SCRATCH = {
    "xs": ("sbuf", [128, N * TK], "float32"),
    "cm": ("sbuf", [128, 128], "float32"),
    "er": ("sbuf", [128, TK], "float32"),
    "pn": ("sbuf", [128, 1], "float32"),
    "two": ("sbuf", [128, 128], "float32"),
    "zer": ("sbuf", [128, 128], "float32"),
    "one": ("sbuf", [128, 1], "float32"),
    "lrow": ("sbuf", [128, 128], "float32"),
    "frow": ("sbuf", [128, 128], "float32"),
    "nl": ("sbuf", [128, 1], "float32"),
    "w0": ("sbuf", [128, 1], "float32"),
    "rc": ("sbuf", [128, 1], "float32"),
    "tt": ("sbuf", [128, 1], "float32"),
    "wc": ("sbuf", [128, 1], "float32"),
    "kc": ("sbuf", [128, 128], "float32"),
    "ph": ("sbuf", [128, TK], "float32"),
    "ss": ("sbuf", [128, TK], "float32"),
    "sq": ("sbuf", [128, TK], "float32"),
    "ys": ("sbuf", [128, TK], "float32"),
    "ps": ("psum", [128, 512], "float32"),
    "pv": ("psum", [128, 512], "float32"),
    "pr": ("psum", [128, 512], "float32"),
    "pc": ("psum", [128, 512], "float32"),
    "pf": ("psum", [128, 512], "float32"),
}
SEMAPHORES = ["ld", "st", "sent", "arr0", "arr1", "arr2", "arr3", "cst", "iod", "expd", "rw", "fr", "sc", "tp", "tp2",
              "nld", "rcd", "ttd", "wcd", "kcd", "a1", "a2", "s", "sqd", "m1", "hd", "m2", "yd"]


def _bits(mask):
    return [e for e in range(mask.bit_length()) if (mask >> e) & 1]


def _mask(engines):
    m = 0
    for e in engines:
        m |= 1 << e
    return m


def _pow2(n):
    p = 1
    while p * 2 <= n:
        p *= 2
    return p


def _plan(src, cores, topo):
    others = [d for d in cores if d != src and topo.may_write(src, d)]
    near = [d for d in others if topo.host(d) == topo.host(src) and topo.chip(d) == topo.chip(src)]
    far = [d for d in others if d not in near]
    far.sort(key=lambda d: (topo.die(d) != topo.die(src), d))
    out = topo.mask(src, far[0])
    for d in far:
        out &= topo.mask(src, d)
    eng = _bits(out)
    k = _pow2(len(eng) // len(far))
    far_plan = [(d, _mask(eng[i * k:(i + 1) * k])) for i, d in enumerate(far)]
    near_plan = []
    for d in near:
        rest = [e for e in _bits(topo.mask(src, d)) if e not in eng]
        near_plan.append((d, _mask(rest[:_pow2(len(rest))])))
    return far_plan, near_plan


def rank_program(g, core, T, topo):
    rank = T.rank_of(core)
    if rank is None:
        return
    S = T.sem
    cores = list(T.cores)
    far, near = _plan(core, cores, topo)

    def slot(r):
        return T.xs[:, r * TK:(r + 1) * TK]

    def landed(d):
        f, n = _plan(d, cores, topo)
        m = dict(f + n)[core]
        return S["arr%d" % T.rank_of(d)], len(_bits(m))

    mine = slot(rank)
    add, mult = AluOpType.add, AluOpType.mult
    Exp, Square = ActivationFunctionType.Exp, ActivationFunctionType.Square
    v, a, pe = g.vector, g.scalar, g.tensor

    g.sync.dma_start(mine, T.x[:]).then_inc(S.ld, 16)

    g.iota(T.pn[:], [[0, 1]], 0, 1, allow_small_or_imprecise_dtypes=True).then_inc(S.iod, 1)
    g.wait_ge(S.ld, 16)
    sent = 0
    trs = []
    for d, m in far:
        rid, pid = topo.addr(d, core)
        trs.append(RemoteDMATransfer(dst_ids=[DstId(rid=rid, pnc=pid)], dma_engine_mask=m,
                                     remote_sem=S["arr%d" % rank], src=mine, dst=mine))
        sent += len(_bits(m))
    g.remote_dma_fused(trs, local_sem=S.sent)
    for d, m in near:
        rid, pid = topo.addr(d, core)
        g.remote_dma(mine, mine, S["arr%d" % rank], S.sent, pid, rid, m)
        sent += len(_bits(m))
    g.wait_ge(S.sent, sent)

    s_run = T.ps[:, 0:TK]
    pv, pr = T.pv[:, 0:TK], T.pr[:, 0:TK]
    nt = len(TAIL)
    v.memset(T.cm[:], 1.0 / 128.0).then_inc(S.cst, 1)
    v.memset(T.er[0:1, :], 128.0 * EPS * K * K).then_inc(S.cst, 1)
    v.memset(T.two[0:1, :], 2.0).then_inc(S.rw, 1)
    v.memset(T.zer[0:1, :], 0.0).then_inc(S.rw, 1)
    v.memset(T.one[0:1, :], 1.0).then_inc(S.rw, 1)
    v.memset(T.frow[0:1, nt:128], 128.0).then_inc(S.fr, 1)
    for i, t in enumerate(TAIL):
        v.memset(T.frow[0:1, i:i + 1], 128.0 * t).then_inc(S.fr, 1)
    v.wait_ge(S.rw, 3)
    v.tensor_tensor_scan(T.lrow[0:1, :], T.two[0:1, :], T.zer[0:1, :], -(2.0 ** (J0 + 2 * KE - 1)), mult, add).then_inc(S.sc, 1)
    pe.wait_ge(S.cst, 2)
    pe.matmul(pv, T.cm[0:1, :], T.er[0:1, :], True, False)
    pe.wait_ge(S.rw, 3)
    pe.wait_ge(S.sc, 1)
    pe.matmul(T.pc[:, 0:1], T.lrow[0:1, :], T.one[0:1, :], True, True).then_inc(S.tp, 1)
    pe.wait_ge(S.fr, nt + 1)
    pe.matmul(T.pf[:, 0:1], T.frow[0:1, :], T.one[0:1, :], True, True).then_inc(S.tp2, 1)
    a.wait_ge(S.iod, 1)
    a.activation(T.w0[:], T.pn[:], Exp, bias=math.log(C) + 0.5 * J0 * LN2, scale=0.5 * LN2).then_inc(S.expd, 1)
    v.wait_ge(S.tp, 1)
    v.tensor_copy(T.nl[:], T.pc[:, 0:1]).then_inc(S.nld, 1)
    v.wait_ge(S.expd, 1)
    v.reciprocal(T.rc[:], T.w0[:]).then_inc(S.rcd, 1)
    v.wait_ge(S.rcd, 1)
    v.wait_ge(S.nld, 1)
    v.tensor_scalar(T.tt[:], T.nl[:], T.rc[:], -0.5 * C * C * K * K, mult, mult).then_inc(S.ttd, 1)
    v.wait_ge(S.ttd, 1)
    v.tensor_scalar(T.wc[:], T.w0[:], 0.5, T.tt[:], mult, add).then_inc(S.wcd, 1)
    v.wait_ge(S.wcd, 1)
    v.wait_ge(S.tp2, 1)
    v.wait_ge(S.cst, 2)
    v.tensor_scalar(T.kc[:], T.cm[:], T.wc[:], T.pf[:, 0:1], mult, mult).then_inc(S.kcd, 1)

    order = [d for d, _ in near] + [d for d, _ in far]
    steps = [S.a1, S.a2, S.s]
    v.wait_ge(S.ld, 16)
    prev = None
    for i, d in enumerate(order):
        sem, cnt = landed(d)
        v.wait_ge(sem, cnt)
        if prev is not None:
            v.wait_ge(prev, 1)
        v.tensor_tensor(T.ss[:] if i == len(order) - 1 else s_run, mine if i == 0 else s_run,
                        slot(T.rank_of(d)), add).then_inc(steps[i], 1)
        prev = steps[i]

    a.wait_ge(S.s, 1)
    a.activation(T.sq[:], T.ss[:], Square, scale=K).then_inc(S.sqd, 1)
    pe.wait_ge(S.sqd, 1)
    pe.matmul(pv, T.cm[:], T.sq[:], False, True).then_inc(S.m1, 1)
    a.wait_ge(S.nld, 1)
    a.wait_ge(S.m1, 1)
    a.activation(T.ph[:], pv, Exp, scale=T.nl[:]).then_inc(S.hd, 1)
    pe.wait_ge(S.kcd, 1)
    pe.wait_ge(S.hd, 1)
    pe.matmul(pr, T.kc[:], T.ph[:], True, True).then_inc(S.m2, 1)
    v.wait_ge(S.m2, 1)
    v.wait_ge(S.s, 1)
    v.tensor_tensor(T.ys[:], pr, T.ss[:], mult).then_inc(S.yd, 1)

    g.sync.wait_ge(S.yd, 1)
    g.sync.dma_start(T.y[:], T.ys[:]).then_inc(S.st, 16)
    g.sync.wait_ge(S.st, 16)
